import numpy as np
import ml_dtypes


def mxq(x, axis, fmt="e4m3"):
    dtype, down = {"e4m3": (ml_dtypes.float8_e4m3fn, 7), "e5m2": (ml_dtypes.float8_e5m2, 14)}[fmt]
    v = np.moveaxis(np.asarray(x, np.float32).astype(ml_dtypes.bfloat16).astype(np.float64), axis, -1)
    blocks = v.reshape(v.shape[:-1] + (-1, 32))
    amax = np.abs(blocks).max(-1, keepdims=True)
    byte = np.maximum(np.where(amax > 0, np.frexp(amax)[1] - 1 + 127, 0) - down, 1)
    scale = np.exp2(byte - 127.0)
    codes = (blocks / scale).astype(np.float32).astype(dtype).astype(np.float64)
    return np.moveaxis((codes * scale).reshape(v.shape), -1, axis)


WIDE = False


def mx_kscale(k):
    if not WIDE:
        return np.ones(k)
    levels = np.array([10, -10, 5, -5, 0])
    if k % 512:
        return np.exp2(np.random.permutation(np.resize(levels, k // 32))).repeat(32)
    a = np.empty((k // 512, 16))
    for p in range(k // 512):
        a[p, :8] = np.random.permutation(np.resize(levels, 8))
        for g in range(8):
            far = levels[np.abs(levels - a[p, g]) >= 10]
            a[p, g + 8] = far[np.random.randint(len(far))]
    return np.exp2(a.ravel()).repeat(32)


def f64(x):
    return np.asarray(x).astype(np.float64)


def striped(idx):
    return np.tile(idx.reshape(-1, 16).T, (8, 1)).astype(np.uint16)


def unstriped(offs):
    return offs[:16].T.reshape(-1).astype(np.int64)


def pack_weight(w):
    k, n = w.shape
    w = f64(np.asarray(w, np.float32).astype(ml_dtypes.bfloat16)).reshape(k // 32, 32, n)
    amax = np.abs(w).max(1)
    byte = np.clip(np.where(amax > 0, np.frexp(amax)[1] - 1 + 127 - 7, 1), 1, 254)
    scaled = (w * np.exp2(127.0 - byte)[:, None, :]).reshape(k, n).astype(np.float32)
    words = np.ascontiguousarray(scaled.reshape(k // 512, 128, 4, n).transpose(0, 1, 3, 2)).astype(ml_dtypes.float8_e4m3fn).view(np.uint8)
    return words, np.ascontiguousarray(byte.astype(np.uint8).reshape(k // 512, 16, n))


def unpack_weight(words, scales):
    g, p, n, _ = words.shape
    vals = np.ascontiguousarray(words).view(ml_dtypes.float8_e4m3fn).astype(np.float64) * np.repeat(np.exp2(scales.astype(np.float64) - 127.0), 8, axis=1)[..., None]
    return vals.transpose(0, 1, 3, 2).reshape(g * 512, n)


def relu(v):
    return np.maximum(v, 0.0)


def sigmoid(v):
    return 1.0 / (1.0 + np.exp(-np.maximum(v, -700.0)))


K, T, S, V, D = 512, 2048, 512, 256, 4
P = 2 ** 7


def setup_inputs():
    n = np.random.standard_normal
    s = mx_kscale(K)[:, None]
    packed_xT = pack_weight(n((K, T)) * s)
    return {
        "x_words": packed_xT[0],
        "x_scales": packed_xT[1],
        "hT": (n((K, V)) / np.sqrt(K) / s).astype(np.float32),
        "ment": (np.tile(0.5 * n(T), (P, 1))).astype(np.float32),
        "gold": (np.tile((np.random.uniform(size=S) < 0.4) * 0.98 + 0.01, (P, 1))).astype(np.float32),
        "offs": striped(np.random.permutation(T)[:S]),
    }


def reference(x_words, x_scales, hT, ment, gold, offs):
    hTq = mxq(f64(hT), 0, "e4m3")
    xq = unpack_weight(x_words, x_scales)[:, unstriped(offs)]
    y = (hTq.T @ xq) + f64(ment)[:1][:, unstriped(offs)]
    top = relu(y.reshape(len(y), -1, D).max(axis=2))
    ex = np.exp(y - np.repeat(top, D, axis=1))
    tot = ex.reshape(len(ex), -1, D).sum(axis=2) + np.exp(-1.0 * top)
    pg = (ex / np.repeat(tot, D, axis=1)) * (sigmoid(4.0 * f64(gold)[:1]))
    return pg.reshape(len(pg), -1, D).sum(axis=2) - (np.exp(-1.0 * top) / tot)

@@ -1,0 +1,189 @@
+from contextlib import ExitStack
+
+import concourse.mybir as mybir
+from concourse.masks import make_identity
+
+K, T, S, V, D = 512, 2048, 512, 256, 4
+P = 128
+G = S // D
+HALF = 128
+SC0 = P - 16
+CLEAR_V, CLEAR_S = 768, 256
+FLOPS = 2 * K * V * S
+
+F32 = mybir.dt.float32
+BF16 = mybir.dt.bfloat16
+I32 = mybir.dt.int32
+U32 = mybir.dt.uint32
+U16 = mybir.dt.uint16
+U8 = mybir.dt.uint8
+FP8X4 = mybir.dt.float8_e4m3fn_x4
+ALU = mybir.AluOpType
+ACT = mybir.ActivationFunctionType
+
+
+def tile_picked_ycoref_net_p_kernel(tc, x_words, x_scales, hT, ment, gold, offs, out):
+    nc = tc.nc
+    halves = range(V // HALF)
+    with ExitStack() as ctx:
+        sb = ctx.enter_context(tc.tile_pool(name="sb", bufs=1))
+        ps = ctx.enter_context(tc.psum_pool(name="ps", bufs=1))
+
+        offsets = sb.tile([P, S // 16], U16, name="offsets")
+        words = sb.tile([P, T], I32, name="words", align_bytes=64)
+        scales = sb.tile([P, T], U8, name="scales", align_bytes=64)
+        ment_row = sb.tile([P, T], F32, name="ment_row", align_bytes=64)
+        marks = sb.tile([P, D], F32, name="marks")
+        h_raw = [sb.tile([P, 4, HALF], F32, name=f"h_raw{h}") for h in halves]
+        ident = sb.tile([P, P], F32, name="ident")
+
+        h_rows = hT.rearrange("(p j) t -> p j t", j=4)
+        scale_rows = x_scales[0].bitcast(I32)
+
+        x_sc = sb.tile([P, D, G], U8, name="x_sc", align_bytes=64)
+        zero = sb.tile([P, 8], F32, name="zero")
+        nc.vector.memset(zero[:], 0.0)
+        nc.vector.memset(scales[0:SC0, :].bitcast(I32), 0)
+        nc.vector.memset(ment_row[0 : P - 1, 0:CLEAR_V], 0.0)
+        nc.vector.memset(x_sc[:].rearrange("p d g -> p (d g)").bitcast(I32), 0)
+        nc.gpsimd.memset(ment_row[0 : P - 1, CLEAR_V : T - CLEAR_S], 0.0)
+        nc.scalar.activation(
+            ment_row[0 : P - 1, T - CLEAR_S : T], zero[0 : P - 1, 0:1].to_broadcast([P - 1, CLEAR_S]), ACT.Copy
+        )
+        make_identity(nc, ident[:])
+
+        nc.sync.dma_start(scales[SC0:P, :].bitcast(I32), scale_rows)
+        nc.sync.dma_start(ment_row[P - 1 : P, :], ment[0:1, :])
+        nc.sync.dma_start(offsets[:], offs)
+        nc.sync.dma_start(h_raw[0][:], h_rows[:, :, 0:HALF])
+        nc.sync.dma_start(words[:], x_words[0].rearrange("p n r -> p (n r)").bitcast(I32))
+        nc.sync.dma_start(h_raw[1][:], h_rows[:, :, HALF:V])
+        nc.sync.dma_start(marks[:], gold[0, :].rearrange("(g d) -> g d", d=D))
+
+        h_bf = [sb.tile([P, HALF, 4], BF16, name=f"h_bf{h}", align_bytes=64) for h in halves]
+        h_codes = [sb.tile([P, HALF], U32, name=f"h_codes{h}", align_bytes=64) for h in halves]
+        h_scales = [sb.tile([P, HALF], U8, name=f"h_scales{h}", align_bytes=64) for h in halves]
+
+        def quantize(h):
+            nc.vector.quantize_mx(
+                out=h_codes[h][:].bitcast(FP8X4),
+                scales=h_scales[h][:],
+                in_=h_bf[h][:].rearrange("p t j -> p (t j)"),
+            )
+
+        sc_picked = sb.tile([P, D, G], U8, name="sc_picked", align_bytes=64)
+        nc.vector.tensor_copy(sc_picked[:].rearrange("p d g -> p g d"), scales[:].indirect(offsets[:]))
+        sc_src = sc_picked[:].rearrange("p d g -> p (d g)").bitcast(I32)
+        sc_dst = x_sc[:].rearrange("p d g -> p (d g)").bitcast(I32)
+        for q in range(4):
+            nc.sync.dma_start(sc_dst[32 * q : 32 * q + 4, :], sc_src[SC0 + 4 * q : SC0 + 4 * q + 4, :])
+        nc.vector.tensor_copy(h_bf[0][:], h_raw[0][:].rearrange("p j t -> p t j"))
+        quantize(0)
+
+        ment_picked = sb.tile([P, S], F32, name="ment_picked")
+        nc.scalar.activation(ment_picked[:], ment_row[:].indirect(offsets[:]), ACT.Copy)
+        ment_ps = ps.tile([P, D, P], F32, name="ment_ps")
+        for d in range(D):
+            nc.tensor.transpose(ment_ps[:, d, :], ment_picked[:].rearrange("p (g d) -> p d g", d=D)[:, d, :], ident[:])
+        m = sb.tile([P, D], F32, name="m")
+        nc.scalar.copy(m[:], ment_ps[:, :, P - 1])
+
+        x_w = sb.tile([P, D, G], U32, name="x_w", align_bytes=64)
+        nc.vector.tensor_copy(x_w[:].rearrange("p d g -> p g d"), words[:].bitcast(U32).indirect(offsets[:]))
+        nc.scalar.copy(h_bf[1][:], h_raw[1][:].rearrange("p j t -> p t j"))
+        quantize(1)
+
+        th = sb.tile([P, D], F32, name="th")
+        w = sb.tile([P, D], F32, name="w")
+        nc.scalar.activation(th[:], marks[:], ACT.Tanh, scale=2.0)
+        nc.gpsimd.tensor_scalar(w[:], th[:], 0.5, 0.5, ALU.mult, ALU.add)
+
+        sc = [ps.tile([P, D, HALF], F32, name=f"sc{h}") for h in halves]
+        run = [sb.tile([P, D, HALF], F32, name=f"run{h}") for h in halves]
+        z = [sb.tile([P, D, HALF], F32, name=f"z{h}") for h in halves]
+        e = [sb.tile([P, D + 1, HALF], F32, name=f"e{h}") for h in halves]
+        a = [sb.tile([P, D + 1, HALF], F32, name=f"a{h}") for h in halves]
+
+        def scores(h):
+            for d in range(D):
+                nc.tensor.matmul_mx(
+                    out=sc[h][:, d, :],
+                    lhsT=x_w[:, d, :].bitcast(FP8X4),
+                    lhsT_scale=x_sc[:, d, :],
+                    rhs=h_codes[h][:].bitcast(FP8X4),
+                    rhs_scale=h_scales[h][:],
+                    start=True,
+                    stop=True,
+                )
+
+        def largest(h, d):
+            if d == 0:
+                nc.vector.tensor_scalar(run[h][:, 0, :], sc[h][:, 0, :], m[:, 0:1], 0.0, ALU.add, ALU.max)
+            else:
+                nc.vector.scalar_tensor_tensor(
+                    run[h][:, d, :], sc[h][:, d, :], m[:, d : d + 1], run[h][:, d - 1, :], ALU.add, ALU.max
+                )
+
+        def shift(h):
+            top2 = run[h][:, D - 1 : D, :].to_broadcast([P, 2, HALF])
+            for d in (0, 2):
+                nc.vector.tensor_tensor(z[h][:, d : d + 2, :], sc[h][:, d : d + 2, :], top2, ALU.subtract)
+
+        def exps(h):
+            nc.scalar.activation(e[h][:, D, :], run[h][:, D - 1, :], ACT.Exp, scale=-1.0)
+            nc.gpsimd.tensor_scalar(a[h][:, D, :], e[h][:, D, :], -1.0, 0.0, ALU.mult, ALU.add)
+            for d in range(D):
+                nc.scalar.activation(e[h][:, d, :], z[h][:, d, :], ACT.Exp, bias=m[:, d : d + 1])
+            for d in range(2):
+                nc.gpsimd.tensor_scalar(a[h][:, d, :], e[h][:, d, :], w[:, d : d + 1], 0.0, ALU.mult, ALU.add)
+
+        def weigh(h):
+            for d in range(2, D):
+                nc.scalar.activation(a[h][:, d, :], e[h][:, d, :], ACT.Copy, scale=w[:, d : d + 1])
+
+        def turned_sum(acc, terms):
+            order = (D, 0, 1, 2, 3)
+            for i, d in enumerate(order):
+                nc.tensor.matmul(acc, terms[:, d, :], ident[:], start=(i == 0), stop=(i == D), is_transpose=True)
+
+        tot = [ps.tile([P, 2, G // 2], F32, name=f"tot{h}") for h in halves]
+        num = [ps.tile([P, 2, G // 2], F32, name=f"num{h}") for h in halves]
+
+        def sum_tot(h):
+            turned_sum(tot[h][:].rearrange("p s g -> p (s g)"), e[h])
+
+        def sum_num(h):
+            turned_sum(num[h][:].rearrange("p s g -> p (s g)"), a[h])
+
+        def finish(h):
+            prod = sb.tile([P, G // 2], F32, name=f"prod{h}")
+            inv = sb.tile([P, 1, G // 2], F32, name=f"inv{h}")
+            other = sb.tile([P, 2, G // 2], F32, name=f"other{h}")
+            cross = sb.tile([P, 2, G // 2], F32, name=f"cross{h}")
+            res = sb.tile([P, 2, G // 2], F32, name=f"res{h}")
+            nc.vector.tensor_reduce(prod[:], tot[h][:].rearrange("p s g -> p g s"), mybir.AxisListType.X, ALU.mult)
+            for side in range(2):
+                nc.scalar.copy(other[:, side, :], tot[h][:, 1 - side, :])
+            nc.vector.reciprocal(inv[:, 0, :], prod[:])
+            nc.vector.tensor_tensor(cross[:], num[h][:], other[:], ALU.mult)
+            nc.vector.tensor_tensor(res[:], cross[:], inv[:].to_broadcast([P, 2, G // 2]), ALU.mult)
+            nc.sync.dma_start(out[h * HALF : (h + 1) * HALF, :], res[:].rearrange("p s g -> p (s g)"))
+
+        scores(0)
+        scores(1)
+        for d in range(D):
+            largest(0, d)
+        shift(0)
+        for d in range(D):
+            largest(1, d)
+        exps(0)
+        shift(1)
+        sum_tot(0)
+        weigh(0)
+        exps(1)
+        sum_num(0)
+        sum_tot(1)
+        weigh(1)
+        finish(0)
+        sum_num(1)
+        finish(1)

@@ -82,7 +82,7 @@ def tile_picked_ycoref_net_p_kernel(tc, x_words, x_scales, hT, ment, gold, offs,
 
         ment_picked = sb.tile([P, S], F32, name="ment_picked")
         nc.scalar.activation(ment_picked[:], ment_row[:].indirect(offsets[:]), ACT.Copy)
-        ment_ps = ps.tile([P, D, P], F32, name="ment_ps")
+        ment_ps = ps.tile([P, D, P], F32, name="ment_ps", tag="shared_bank")
         for d in range(D):
             nc.tensor.transpose(ment_ps[:, d, :], ment_picked[:].rearrange("p (g d) -> p d g", d=D)[:, d, :], ident[:])
         m = sb.tile([P, D], F32, name="m")
@@ -98,16 +98,20 @@ def tile_picked_ycoref_net_p_kernel(tc, x_words, x_scales, hT, ment, gold, offs,
         nc.scalar.activation(th[:], marks[:], ACT.Tanh, scale=2.0)
         nc.gpsimd.tensor_scalar(w[:], th[:], 0.5, 0.5, ALU.mult, ALU.add)
 
-        sc = [ps.tile([P, D, HALF], F32, name=f"sc{h}") for h in halves]
-        run = [sb.tile([P, D, HALF], F32, name=f"run{h}") for h in halves]
+        lo = [ps.tile([P, 2, HALF], F32, name=f"lo{h}") for h in halves]
+        hi = [ps.tile([P, 2, HALF], F32, name=f"hi{h}") for h in halves]
+        y = [sb.tile([P, 2, HALF], F32, name=f"y{h}") for h in halves]
+        u = [sb.tile([P, 2, HALF], F32, name=f"u{h}") for h in halves]
+        top = [sb.tile([P, 1, HALF], F32, name=f"top{h}") for h in halves]
         z = [sb.tile([P, D, HALF], F32, name=f"z{h}") for h in halves]
         e = [sb.tile([P, D + 1, HALF], F32, name=f"e{h}") for h in halves]
         a = [sb.tile([P, D + 1, HALF], F32, name=f"a{h}") for h in halves]
 
         def scores(h):
             for d in range(D):
+                bank = lo[h] if d < 2 else hi[h]
                 nc.tensor.matmul_mx(
-                    out=sc[h][:, d, :],
+                    out=bank[:, d % 2, :],
                     lhsT=x_w[:, d, :].bitcast(FP8X4),
                     lhsT_scale=x_sc[:, d, :],
                     rhs=h_codes[h][:].bitcast(FP8X4),
@@ -116,44 +120,59 @@ def tile_picked_ycoref_net_p_kernel(tc, x_words, x_scales, hT, ment, gold, offs,
                     stop=True,
                 )
 
-        def largest(h, d):
-            if d == 0:
-                nc.vector.tensor_scalar(run[h][:, 0, :], sc[h][:, 0, :], m[:, 0:1], 0.0, ALU.add, ALU.max)
-            else:
+        def largest(h):
+            for d in range(2):
+                nc.scalar.activation(y[h][:, d, :], lo[h][:, d, :], ACT.Relu, bias=m[:, d : d + 1])
+            for d in range(2):
                 nc.vector.scalar_tensor_tensor(
-                    run[h][:, d, :], sc[h][:, d, :], m[:, d : d + 1], run[h][:, d - 1, :], ALU.add, ALU.max
+                    u[h][:, d, :], hi[h][:, d, :], m[:, 2 + d : 3 + d], y[h][:, d, :], ALU.add, ALU.max
                 )
+            nc.vector.tensor_tensor(top[h][:, 0, :], u[h][:, 0, :], u[h][:, 1, :], ALU.max)
 
         def shift(h):
-            top2 = run[h][:, D - 1 : D, :].to_broadcast([P, 2, HALF])
-            for d in (0, 2):
-                nc.vector.tensor_tensor(z[h][:, d : d + 2, :], sc[h][:, d : d + 2, :], top2, ALU.subtract)
+            top2 = top[h][:].to_broadcast([P, 2, HALF])
+            nc.vector.tensor_tensor(z[h][:, 0:2, :], lo[h][:], top2, ALU.subtract)
+            nc.vector.tensor_tensor(z[h][:, 2:4, :], hi[h][:], top2, ALU.subtract)
 
         def exps(h):
-            nc.scalar.activation(e[h][:, D, :], run[h][:, D - 1, :], ACT.Exp, scale=-1.0)
-            nc.gpsimd.tensor_scalar(a[h][:, D, :], e[h][:, D, :], -1.0, 0.0, ALU.mult, ALU.add)
+            nc.scalar.activation(e[h][:, D, :], top[h][:, 0, :], ACT.Exp, scale=-1.0)
             for d in range(D):
                 nc.scalar.activation(e[h][:, d, :], z[h][:, d, :], ACT.Exp, bias=m[:, d : d + 1])
-            for d in range(2):
-                nc.gpsimd.tensor_scalar(a[h][:, d, :], e[h][:, d, :], w[:, d : d + 1], 0.0, ALU.mult, ALU.add)
 
-        def weigh(h):
-            for d in range(2, D):
+        def weigh_scalar(h, ds):
+            for d in ds:
                 nc.scalar.activation(a[h][:, d, :], e[h][:, d, :], ACT.Copy, scale=w[:, d : d + 1])
 
-        def turned_sum(acc, terms):
-            order = (D, 0, 1, 2, 3)
+        def weigh_vector(h):
+            nc.vector.scalar_tensor_tensor(a[h][:, 0, :], e[h][:, 0, :], w[:, 0:1], e[h][:, D, :], ALU.mult, ALU.subtract)
+            nc.vector.scalar_tensor_tensor(a[h][:, 1, :], e[h][:, 1, :], w[:, 1:2], a[h][:, 0, :], ALU.mult, ALU.add)
+
+        def weigh_gpsimd(h):
+            nc.gpsimd.tensor_scalar(a[h][:, D, :], e[h][:, D, :], -1.0, 0.0, ALU.mult, ALU.add)
+            nc.gpsimd.tensor_scalar(a[h][:, 0, :], e[h][:, 0, :], w[:, 0:1], 0.0, ALU.mult, ALU.add)
+
+        def turned_sum(acc, terms, order):
             for i, d in enumerate(order):
-                nc.tensor.matmul(acc, terms[:, d, :], ident[:], start=(i == 0), stop=(i == D), is_transpose=True)
+                nc.tensor.matmul(acc, terms[:, d, :], ident[:], start=(i == 0), stop=(i == len(order) - 1), is_transpose=True)
 
         tot = [ps.tile([P, 2, G // 2], F32, name=f"tot{h}") for h in halves]
-        num = [ps.tile([P, 2, G // 2], F32, name=f"num{h}") for h in halves]
+        num = [
+            ps.tile([P, 2, G // 2], F32, name="num0"),
+            ps.tile([P, 2, G // 2], F32, name="num1", tag="shared_bank"),
+        ]
 
         def sum_tot(h):
-            turned_sum(tot[h][:].rearrange("p s g -> p (s g)"), e[h])
+            turned_sum(tot[h][:].rearrange("p s g -> p (s g)"), e[h], (D, 0, 1, 2, 3))
 
-        def sum_num(h):
-            turned_sum(num[h][:].rearrange("p s g -> p (s g)"), a[h])
+        def sum_num(h, order):
+            turned_sum(num[h][:].rearrange("p s g -> p (s g)"), a[h], order)
+
+        def finish_plain(h):
+            inv = sb.tile([P, 2, G // 2], F32, name=f"inv{h}")
+            res = sb.tile([P, 2, G // 2], F32, name=f"res{h}")
+            nc.vector.reciprocal(inv[:], tot[h][:])
+            nc.vector.tensor_tensor(res[:], num[h][:], inv[:], ALU.mult)
+            nc.sync.dma_start(out[h * HALF : (h + 1) * HALF, :], res[:].rearrange("p s g -> p (s g)"))
 
         def finish(h):
             prod = sb.tile([P, G // 2], F32, name=f"prod{h}")
@@ -171,19 +190,19 @@ def tile_picked_ycoref_net_p_kernel(tc, x_words, x_scales, hT, ment, gold, offs,
 
         scores(0)
         scores(1)
-        for d in range(D):
-            largest(0, d)
+        largest(0)
         shift(0)
-        for d in range(D):
-            largest(1, d)
+        largest(1)
         exps(0)
         shift(1)
         sum_tot(0)
-        weigh(0)
         exps(1)
-        sum_num(0)
         sum_tot(1)
-        weigh(1)
+        weigh_gpsimd(1)
+        weigh_vector(0)
+        weigh_scalar(0, (2, 3))
+        sum_num(0, (2, 3, 1))
+        weigh_scalar(1, (1, 2, 3))
         finish(0)
-        sum_num(1)
-        finish(1)
+        sum_num(1, (D, 0, 1, 2, 3))
+        finish_plain(1)

@@ -41,6 +41,7 @@ def tile_picked_ycoref_net_p_kernel(tc, x_words, x_scales, hT, ment, gold, offs,
         scale_rows = x_scales[0].bitcast(I32)
 
         x_sc = sb.tile([P, D, G], U8, name="x_sc", align_bytes=64)
+        nc.scalar.dma_start(ment_row[P - 1 : P, :], ment[0:1, :])
         zero = sb.tile([P, 8], F32, name="zero")
         nc.vector.memset(zero[:], 0.0)
         nc.vector.memset(scales[0:SC0, :].bitcast(I32), 0)
@@ -53,7 +54,6 @@ def tile_picked_ycoref_net_p_kernel(tc, x_words, x_scales, hT, ment, gold, offs,
         make_identity(nc, ident[:])
 
         nc.sync.dma_start(scales[SC0:P, :].bitcast(I32), scale_rows)
-        nc.sync.dma_start(ment_row[P - 1 : P, :], ment[0:1, :])
         nc.sync.dma_start(offsets[:], offs)
         nc.sync.dma_start(h_raw[0][:], h_rows[:, :, 0:HALF])
         nc.sync.dma_start(words[:], x_words[0].rearrange("p n r -> p (n r)").bitcast(I32))
@@ -127,12 +127,14 @@ def tile_picked_ycoref_net_p_kernel(tc, x_words, x_scales, hT, ment, gold, offs,
                 nc.vector.scalar_tensor_tensor(
                     u[h][:, d, :], hi[h][:, d, :], m[:, 2 + d : 3 + d], y[h][:, d, :], ALU.add, ALU.max
                 )
+
+        def join(h):
             nc.vector.tensor_tensor(top[h][:, 0, :], u[h][:, 0, :], u[h][:, 1, :], ALU.max)
 
-        def shift(h):
-            top2 = top[h][:].to_broadcast([P, 2, HALF])
-            nc.vector.tensor_tensor(z[h][:, 0:2, :], lo[h][:], top2, ALU.subtract)
-            nc.vector.tensor_tensor(z[h][:, 2:4, :], hi[h][:], top2, ALU.subtract)
+        def shift(h, d0, d1):
+            bank = lo[h] if d0 < 2 else hi[h]
+            wide = top[h][:].to_broadcast([P, d1 - d0, HALF])
+            nc.vector.tensor_tensor(z[h][:, d0:d1, :], bank[:, d0 % 2 : d0 % 2 + d1 - d0, :], wide, ALU.subtract)
 
         def exps(h):
             nc.scalar.activation(e[h][:, D, :], top[h][:, 0, :], ACT.Exp, scale=-1.0)
@@ -174,27 +176,19 @@ def tile_picked_ycoref_net_p_kernel(tc, x_words, x_scales, hT, ment, gold, offs,
             nc.vector.tensor_tensor(res[:], num[h][:], inv[:], ALU.mult)
             nc.sync.dma_start(out[h * HALF : (h + 1) * HALF, :], res[:].rearrange("p s g -> p (s g)"))
 
-        def finish(h):
-            prod = sb.tile([P, G // 2], F32, name=f"prod{h}")
-            inv = sb.tile([P, 1, G // 2], F32, name=f"inv{h}")
-            other = sb.tile([P, 2, G // 2], F32, name=f"other{h}")
-            cross = sb.tile([P, 2, G // 2], F32, name=f"cross{h}")
-            res = sb.tile([P, 2, G // 2], F32, name=f"res{h}")
-            nc.vector.tensor_reduce(prod[:], tot[h][:].rearrange("p s g -> p g s"), mybir.AxisListType.X, ALU.mult)
-            for side in range(2):
-                nc.scalar.copy(other[:, side, :], tot[h][:, 1 - side, :])
-            nc.vector.reciprocal(inv[:, 0, :], prod[:])
-            nc.vector.tensor_tensor(cross[:], num[h][:], other[:], ALU.mult)
-            nc.vector.tensor_tensor(res[:], cross[:], inv[:].to_broadcast([P, 2, G // 2]), ALU.mult)
-            nc.sync.dma_start(out[h * HALF : (h + 1) * HALF, :], res[:].rearrange("p s g -> p (s g)"))
-
         scores(0)
         scores(1)
         largest(0)
-        shift(0)
+        join(0)
         largest(1)
+        shift(0, 0, 1)
+        shift(0, 1, 2)
+        join(1)
+        shift(0, 2, 4)
         exps(0)
-        shift(1)
+        shift(1, 0, 2)
+        shift(1, 2, 3)
+        shift(1, 3, 4)
         sum_tot(0)
         exps(1)
         sum_tot(1)
@@ -203,6 +197,6 @@ def tile_picked_ycoref_net_p_kernel(tc, x_words, x_scales, hT, ment, gold, offs,
         weigh_scalar(0, (2, 3))
         sum_num(0, (2, 3, 1))
         weigh_scalar(1, (1, 2, 3))
-        finish(0)
+        finish_plain(0)
         sum_num(1, (D, 0, 1, 2, 3))
         finish_plain(1)

@@ -138,6 +138,8 @@ def tile_picked_ycoref_net_p_kernel(tc, x_words, x_scales, hT, ment, gold, offs,
 
         def exps(h):
             nc.scalar.activation(e[h][:, D, :], top[h][:, 0, :], ACT.Exp, scale=-1.0)
+            if h == 0:
+                negate(h)
             for d in range(D):
                 nc.scalar.activation(e[h][:, d, :], z[h][:, d, :], ACT.Exp, bias=m[:, d : d + 1])
 
@@ -145,13 +147,8 @@ def tile_picked_ycoref_net_p_kernel(tc, x_words, x_scales, hT, ment, gold, offs,
             for d in ds:
                 nc.scalar.activation(a[h][:, d, :], e[h][:, d, :], ACT.Copy, scale=w[:, d : d + 1])
 
-        def weigh_vector(h):
-            nc.vector.scalar_tensor_tensor(a[h][:, 0, :], e[h][:, 0, :], w[:, 0:1], e[h][:, D, :], ALU.mult, ALU.subtract)
-            nc.vector.scalar_tensor_tensor(a[h][:, 1, :], e[h][:, 1, :], w[:, 1:2], a[h][:, 0, :], ALU.mult, ALU.add)
-
-        def weigh_gpsimd(h):
-            nc.gpsimd.tensor_scalar(a[h][:, D, :], e[h][:, D, :], -1.0, 0.0, ALU.mult, ALU.add)
-            nc.gpsimd.tensor_scalar(a[h][:, 0, :], e[h][:, 0, :], w[:, 0:1], 0.0, ALU.mult, ALU.add)
+        def negate(h):
+            nc.scalar.activation(a[h][:, D, :], e[h][:, D, :], ACT.Copy, scale=-1.0)
 
         def turned_sum(acc, terms, order):
             for i, d in enumerate(order):
@@ -192,11 +189,10 @@ def tile_picked_ycoref_net_p_kernel(tc, x_words, x_scales, hT, ment, gold, offs,
         sum_tot(0)
         exps(1)
         sum_tot(1)
-        weigh_gpsimd(1)
-        weigh_vector(0)
-        weigh_scalar(0, (2, 3))
-        sum_num(0, (2, 3, 1))
-        weigh_scalar(1, (1, 2, 3))
+        weigh_scalar(0, range(D))
+        sum_num(0, (D, 0, 1, 2, 3))
+        negate(1)
+        weigh_scalar(1, range(D))
         finish_plain(0)
         sum_num(1, (D, 0, 1, 2, 3))
         finish_plain(1)

from contextlib import ExitStack

import concourse.mybir as mybir
from concourse.masks import make_identity

K, T, S, V, D = 512, 2048, 512, 256, 4
P = 128
G = S // D
HALF = 128
SC0 = P - 16
CLEAR_V, CLEAR_S = 768, 256
FLOPS = 2 * K * V * S

F32 = mybir.dt.float32
BF16 = mybir.dt.bfloat16
I32 = mybir.dt.int32
U32 = mybir.dt.uint32
U16 = mybir.dt.uint16
U8 = mybir.dt.uint8
FP8X4 = mybir.dt.float8_e4m3fn_x4
ALU = mybir.AluOpType
ACT = mybir.ActivationFunctionType


def tile_picked_ycoref_net_p_kernel(tc, x_words, x_scales, hT, ment, gold, offs, out):
    nc = tc.nc
    halves = range(V // HALF)
    with ExitStack() as ctx:
        sb = ctx.enter_context(tc.tile_pool(name="sb", bufs=1))
        ps = ctx.enter_context(tc.psum_pool(name="ps", bufs=1))

        offsets = sb.tile([P, S // 16], U16, name="offsets")
        words = sb.tile([P, T], I32, name="words", align_bytes=64)
        scales = sb.tile([P, T], U8, name="scales", align_bytes=64)
        ment_row = sb.tile([P, T], F32, name="ment_row", align_bytes=64)
        marks = sb.tile([P, D], F32, name="marks")
        h_raw = [sb.tile([P, 4, HALF], F32, name=f"h_raw{h}") for h in halves]
        ident = sb.tile([P, P], F32, name="ident")

        h_rows = hT.rearrange("(p j) t -> p j t", j=4)
        scale_rows = x_scales[0].bitcast(I32)

        x_sc = sb.tile([P, D, G], U8, name="x_sc", align_bytes=64)
        nc.scalar.dma_start(ment_row[P - 1 : P, :], ment[0:1, :])
        zero = sb.tile([P, 8], F32, name="zero")
        nc.vector.memset(zero[:], 0.0)
        nc.vector.memset(scales[0:SC0, :].bitcast(I32), 0)
        nc.vector.memset(ment_row[0 : P - 1, 0:CLEAR_V], 0.0)
        nc.vector.memset(x_sc[:].rearrange("p d g -> p (d g)").bitcast(I32), 0)
        nc.gpsimd.memset(ment_row[0 : P - 1, CLEAR_V : T - CLEAR_S], 0.0)
        nc.scalar.activation(
            ment_row[0 : P - 1, T - CLEAR_S : T], zero[0 : P - 1, 0:1].to_broadcast([P - 1, CLEAR_S]), ACT.Copy
        )
        make_identity(nc, ident[:])

        nc.sync.dma_start(scales[SC0:P, :].bitcast(I32), scale_rows)
        nc.sync.dma_start(offsets[:], offs)
        nc.sync.dma_start(h_raw[0][:], h_rows[:, :, 0:HALF])
        nc.sync.dma_start(words[:], x_words[0].rearrange("p n r -> p (n r)").bitcast(I32))
        nc.sync.dma_start(h_raw[1][:], h_rows[:, :, HALF:V])
        nc.sync.dma_start(marks[:], gold[0, :].rearrange("(g d) -> g d", d=D))

        h_bf = [sb.tile([P, HALF, 4], BF16, name=f"h_bf{h}", align_bytes=64) for h in halves]
        h_codes = [sb.tile([P, HALF], U32, name=f"h_codes{h}", align_bytes=64) for h in halves]
        h_scales = [sb.tile([P, HALF], U8, name=f"h_scales{h}", align_bytes=64) for h in halves]

        def quantize(h):
            nc.vector.quantize_mx(
                out=h_codes[h][:].bitcast(FP8X4),
                scales=h_scales[h][:],
                in_=h_bf[h][:].rearrange("p t j -> p (t j)"),
            )

        sc_picked = sb.tile([P, D, G], U8, name="sc_picked", align_bytes=64)
        nc.vector.tensor_copy(sc_picked[:].rearrange("p d g -> p g d"), scales[:].indirect(offsets[:]))
        sc_src = sc_picked[:].rearrange("p d g -> p (d g)").bitcast(I32)
        sc_dst = x_sc[:].rearrange("p d g -> p (d g)").bitcast(I32)
        for q in range(4):
            nc.sync.dma_start(sc_dst[32 * q : 32 * q + 4, :], sc_src[SC0 + 4 * q : SC0 + 4 * q + 4, :])
        nc.vector.tensor_copy(h_bf[0][:], h_raw[0][:].rearrange("p j t -> p t j"))
        quantize(0)

        ment_picked = sb.tile([P, S], F32, name="ment_picked")
        nc.scalar.activation(ment_picked[:], ment_row[:].indirect(offsets[:]), ACT.Copy)
        ment_ps = ps.tile([P, D, P], F32, name="ment_ps", tag="shared_bank")
        for d in range(D):
            nc.tensor.transpose(ment_ps[:, d, :], ment_picked[:].rearrange("p (g d) -> p d g", d=D)[:, d, :], ident[:])
        m = sb.tile([P, D], F32, name="m")
        nc.scalar.copy(m[:], ment_ps[:, :, P - 1])

        x_w = sb.tile([P, D, G], U32, name="x_w", align_bytes=64)
        nc.vector.tensor_copy(x_w[:].rearrange("p d g -> p g d"), words[:].bitcast(U32).indirect(offsets[:]))
        nc.scalar.copy(h_bf[1][:], h_raw[1][:].rearrange("p j t -> p t j"))
        quantize(1)

        th = sb.tile([P, D], F32, name="th")
        w = sb.tile([P, D], F32, name="w")
        nc.scalar.activation(th[:], marks[:], ACT.Tanh, scale=2.0)
        nc.gpsimd.tensor_scalar(w[:], th[:], 0.5, 0.5, ALU.mult, ALU.add)

        lo = [ps.tile([P, 2, HALF], F32, name=f"lo{h}") for h in halves]
        hi = [ps.tile([P, 2, HALF], F32, name=f"hi{h}") for h in halves]
        y = [sb.tile([P, 2, HALF], F32, name=f"y{h}") for h in halves]
        u = [sb.tile([P, 2, HALF], F32, name=f"u{h}") for h in halves]
        top = [sb.tile([P, 1, HALF], F32, name=f"top{h}") for h in halves]
        z = [sb.tile([P, D, HALF], F32, name=f"z{h}") for h in halves]
        e = [sb.tile([P, D + 1, HALF], F32, name=f"e{h}") for h in halves]
        a = [sb.tile([P, D + 1, HALF], F32, name=f"a{h}") for h in halves]

        def scores(h):
            for d in range(D):
                bank = lo[h] if d < 2 else hi[h]
                nc.tensor.matmul_mx(
                    out=bank[:, d % 2, :],
                    lhsT=x_w[:, d, :].bitcast(FP8X4),
                    lhsT_scale=x_sc[:, d, :],
                    rhs=h_codes[h][:].bitcast(FP8X4),
                    rhs_scale=h_scales[h][:],
                    start=True,
                    stop=True,
                )

        def largest(h):
            for d in range(2):
                nc.scalar.activation(y[h][:, d, :], lo[h][:, d, :], ACT.Relu, bias=m[:, d : d + 1])
            for d in range(2):
                nc.vector.scalar_tensor_tensor(
                    u[h][:, d, :], hi[h][:, d, :], m[:, 2 + d : 3 + d], y[h][:, d, :], ALU.add, ALU.max
                )

        def join(h):
            nc.vector.tensor_tensor(top[h][:, 0, :], u[h][:, 0, :], u[h][:, 1, :], ALU.max)

        def shift(h, d0, d1):
            bank = lo[h] if d0 < 2 else hi[h]
            wide = top[h][:].to_broadcast([P, d1 - d0, HALF])
            nc.vector.tensor_tensor(z[h][:, d0:d1, :], bank[:, d0 % 2 : d0 % 2 + d1 - d0, :], wide, ALU.subtract)

        def exps(h):
            nc.scalar.activation(e[h][:, D, :], top[h][:, 0, :], ACT.Exp, scale=-1.0)
            if h == 0:
                negate(h)
            for d in range(D):
                nc.scalar.activation(e[h][:, d, :], z[h][:, d, :], ACT.Exp, bias=m[:, d : d + 1])

        def weigh_scalar(h, ds):
            for d in ds:
                nc.scalar.activation(a[h][:, d, :], e[h][:, d, :], ACT.Copy, scale=w[:, d : d + 1])

        def negate(h):
            nc.scalar.activation(a[h][:, D, :], e[h][:, D, :], ACT.Copy, scale=-1.0)

        def turned_sum(acc, terms, order):
            for i, d in enumerate(order):
                nc.tensor.matmul(acc, terms[:, d, :], ident[:], start=(i == 0), stop=(i == len(order) - 1), is_transpose=True)

        tot = [ps.tile([P, 2, G // 2], F32, name=f"tot{h}") for h in halves]
        num = [
            ps.tile([P, 2, G // 2], F32, name="num0"),
            ps.tile([P, 2, G // 2], F32, name="num1", tag="shared_bank"),
        ]

        def sum_tot(h):
            turned_sum(tot[h][:].rearrange("p s g -> p (s g)"), e[h], (D, 0, 1, 2, 3))

        def sum_num(h, order):
            turned_sum(num[h][:].rearrange("p s g -> p (s g)"), a[h], order)

        def finish_plain(h):
            inv = sb.tile([P, 2, G // 2], F32, name=f"inv{h}")
            res = sb.tile([P, 2, G // 2], F32, name=f"res{h}")
            nc.vector.reciprocal(inv[:], tot[h][:])
            nc.vector.tensor_tensor(res[:], num[h][:], inv[:], ALU.mult)
            nc.sync.dma_start(out[h * HALF : (h + 1) * HALF, :], res[:].rearrange("p s g -> p (s g)"))

        scores(0)
        scores(1)
        largest(0)
        join(0)
        largest(1)
        shift(0, 0, 1)
        shift(0, 1, 2)
        join(1)
        shift(0, 2, 4)
        exps(0)
        shift(1, 0, 2)
        shift(1, 2, 3)
        shift(1, 3, 4)
        sum_tot(0)
        exps(1)
        sum_tot(1)
        weigh_scalar(0, range(D))
        sum_num(0, (D, 0, 1, 2, 3))
        negate(1)
        weigh_scalar(1, range(D))
        finish_plain(0)
        sum_num(1, (D, 0, 1, 2, 3))
        finish_plain(1)
